import numpy as np
import ml_dtypes


def mxq(x, axis, fmt="e4m3"):
    dtype, down = {"e4m3": (ml_dtypes.float8_e4m3fn, 7), "e5m2": (ml_dtypes.float8_e5m2, 14)}[fmt]
    v = np.moveaxis(np.asarray(x, np.float32).astype(ml_dtypes.bfloat16).astype(np.float64), axis, -1)
    blocks = v.reshape(v.shape[:-1] + (-1, 32))
    amax = np.abs(blocks).max(-1, keepdims=True)
    byte = np.maximum(np.where(amax > 0, np.frexp(amax)[1] - 1 + 127, 0) - down, 1)
    scale = np.exp2(byte - 127.0)
    codes = (blocks / scale).astype(np.float32).astype(dtype).astype(np.float64)
    return np.moveaxis((codes * scale).reshape(v.shape), -1, axis)


WIDE = False


def mx_kscale(k):
    if not WIDE:
        return np.ones(k)
    levels = np.array([10, -10, 5, -5, 0])
    if k % 512:
        return np.exp2(np.random.permutation(np.resize(levels, k // 32))).repeat(32)
    a = np.empty((k // 512, 16))
    for p in range(k // 512):
        a[p, :8] = np.random.permutation(np.resize(levels, 8))
        for g in range(8):
            far = levels[np.abs(levels - a[p, g]) >= 10]
            a[p, g + 8] = far[np.random.randint(len(far))]
    return np.exp2(a.ravel()).repeat(32)


def f64(x):
    return np.asarray(x).astype(np.float64)


def striped(idx):
    return np.tile(idx.reshape(-1, 16).T, (8, 1)).astype(np.uint16)


def unstriped(offs):
    return offs[:16].T.reshape(-1).astype(np.int64)


def pack_weight(w):
    k, n = w.shape
    w = f64(np.asarray(w, np.float32).astype(ml_dtypes.bfloat16)).reshape(k // 32, 32, n)
    amax = np.abs(w).max(1)
    byte = np.clip(np.where(amax > 0, np.frexp(amax)[1] - 1 + 127 - 7, 1), 1, 254)
    scaled = (w * np.exp2(127.0 - byte)[:, None, :]).reshape(k, n).astype(np.float32)
    words = np.ascontiguousarray(scaled.reshape(k // 512, 128, 4, n).transpose(0, 1, 3, 2)).astype(ml_dtypes.float8_e4m3fn).view(np.uint8)
    return words, np.ascontiguousarray(byte.astype(np.uint8).reshape(k // 512, 16, n))


def unpack_weight(words, scales):
    g, p, n, _ = words.shape
    vals = np.ascontiguousarray(words).view(ml_dtypes.float8_e4m3fn).astype(np.float64) * np.repeat(np.exp2(scales.astype(np.float64) - 127.0), 8, axis=1)[..., None]
    return vals.transpose(0, 1, 3, 2).reshape(g * 512, n)


K, T, E, C, N = 512, 512, 2, 256, 256


def by_expert(wq, xq):
    return np.concatenate([wq[e].T @ xq[:, e * C:(e + 1) * C] for e in range(E)], axis=1)


def setup_inputs():
    n = np.random.standard_normal
    s = mx_kscale(K)[:, None]
    packed = [pack_weight(m) for m in n((E, K, N)) / np.sqrt(K) / s[None]]
    return {
        "xT": (n((K, T)) * s).astype(np.float32),
        "w_words": np.stack([m[0] for m in packed]),
        "w_scales": np.stack([m[1] for m in packed]),
        "gate": np.tile(np.random.uniform(0.2, 1.0, E * C), (N, 1)).astype(np.float32),
        "offs": striped(np.random.permutation(T)[:E * C]),
    }


def reference(xT, w_words, w_scales, gate, offs):
    idx = unstriped(offs)
    xq = mxq(f64(xT)[:, idx], 0, "e4m3")
    w = np.stack([unpack_weight(w_words[e], w_scales[e]) for e in range(E)])
    y = by_expert(w, xq)
    out = np.zeros((N, T))
    out[:, idx] = f64(gate) * y
    return out

@@ -1,0 +1,127 @@
+from contextlib import ExitStack
+
+import concourse.mybir as mybir
+
+K, T, E, C, N = 512, 512, 2, 256, 256
+FLOPS = 2 * K * N * E * C
+
+F32 = mybir.dt.float32
+BF16 = mybir.dt.bfloat16
+I32 = mybir.dt.int32
+U16 = mybir.dt.uint16
+U8 = mybir.dt.uint8
+FP8X4 = mybir.dt.float8_e4m3fn_x4
+MULT = mybir.AluOpType.mult
+
+P = 128
+PACK = 4
+NB = N // P
+OC = C // 16
+
+
+def tile_routed_moe_kernel(tc, xT, w_words, w_scales, gate, offs, out):
+    nc = tc.nc
+    with ExitStack() as ctx:
+        keep = ctx.enter_context(tc.tile_pool(name="keep", bufs=1))
+        psum = ctx.enter_context(tc.psum_pool(name="psum", bufs=1))
+
+        offsets = keep.tile([P, E * C // 16], U16, name="offsets")
+        nc.sync.dma_start(offsets[:], offs)
+
+        planes_dram = xT.rearrange("(p t) n -> p t n", t=PACK)
+        planes = []
+        for t in range(PACK):
+            plane = keep.tile([P, T], F32, name="plane%d" % t)
+            nc.sync.dma_start(plane[:], planes_dram[:, t, :])
+            planes.append(plane)
+
+        w_plane = keep.tile([P, E, N], U8, name="w_plane", align_bytes=64)
+        nc.vector.memset(w_plane[:].rearrange("p e n -> p (e n)").bitcast(I32), 0)
+        for q in range(4):
+            nc.sync.dma_start(
+                w_plane[32 * q : 32 * q + 4, :, :].bitcast(I32),
+                w_scales[:, 0, 4 * q : 4 * q + 4, :].rearrange("e q n -> q e n").bitcast(I32),
+            )
+        w_codes = keep.tile([P, E, N], I32, name="w_codes", align_bytes=64)
+        nc.sync.dma_start(w_codes[:], w_words.rearrange("e a p n r -> p (e a) (n r)").bitcast(I32))
+
+        gates = keep.tile([P, NB, E * C], F32, name="gates")
+        nc.sync.dma_start(gates[:], gate.rearrange("(b p) j -> p b j", p=P))
+
+        warm_in = keep.tile([P, 1], F32, name="warm_in")
+        warm_out = keep.tile([P, 1], F32, name="warm_out")
+        nc.vector.memset(warm_in[:], 0.0)
+        nc.scalar.copy(warm_out[:], warm_in[:])
+
+        windows = [keep.tile([P, T], F32, name="window%d" % b) for b in range(NB)]
+
+        gathered, grouped, codes, scales, sums, sums_sb = {}, {}, {}, {}, {}, {}
+        for e in range(E):
+            gathered[e] = keep.tile([P, PACK, C], F32, name="gathered%d" % e)
+            grouped[e] = keep.tile([P, C, PACK], BF16, name="grouped%d" % e, align_bytes=64)
+            codes[e] = keep.tile([P, C], I32, name="codes%d" % e, align_bytes=64)
+            scales[e] = keep.tile([P, C], U8, name="scales%d" % e, align_bytes=64)
+            sums[e] = psum.tile([P, NB, C], F32, name="sums%d" % e)
+            for b in range(NB):
+                sums_sb[e, b] = keep.tile([P, C], F32, name="sums_sb%d_%d" % (e, b))
+
+        def slots(e):
+            return offsets[:, e * OC : (e + 1) * OC]
+
+        def gather(e, t):
+            nc.vector.tensor_copy(gathered[e][:, t, :], planes[t][:].indirect(slots(e)))
+
+        def interleave(e):
+            nc.scalar.copy(grouped[e][:], gathered[e][:].rearrange("p t c -> p c t"))
+
+        def quantise(e):
+            nc.vector.quantize_mx(
+                out=codes[e][:].bitcast(FP8X4),
+                scales=scales[e][:],
+                in_=grouped[e][:].rearrange("p c t -> p (c t)"),
+            )
+
+        def multiply(e):
+            for b in range(NB):
+                nc.tensor.matmul_mx(
+                    out=sums[e][:, b, :],
+                    lhsT=w_codes[:, e, b * P : (b + 1) * P].bitcast(FP8X4),
+                    lhsT_scale=w_plane[:, e, b * P : (b + 1) * P],
+                    rhs=codes[e][:].bitcast(FP8X4),
+                    rhs_scale=scales[e][:],
+                    start=True,
+                    stop=True,
+                )
+
+        def empty(e):
+            for b in range(NB):
+                nc.scalar.copy(sums_sb[e, b][:], sums[e][:, b, :])
+
+        def scatter(e, b):
+            nc.vector.tensor_tensor(
+                windows[b][:].indirect(slots(e)),
+                sums_sb[e, b][:],
+                gates[:, b, e * C : (e + 1) * C],
+                MULT,
+            )
+
+        for t in range(PACK):
+            gather(0, t)
+        interleave(0)
+        gather(1, 0)
+        gather(1, 1)
+        quantise(0)
+        multiply(0)
+        gather(1, 2)
+        gather(1, 3)
+        empty(0)
+        interleave(1)
+        scatter(0, 0)
+        quantise(1)
+        multiply(1)
+        empty(1)
+        scatter(0, 1)
+        scatter(1, 0)
+        nc.sync.dma_start(out[0:P, :], windows[0][:])
+        scatter(1, 1)
+        nc.sync.dma_start(out[P : 2 * P, :], windows[1][:])

@@ -12,11 +12,13 @@ U16 = mybir.dt.uint16
 U8 = mybir.dt.uint8
 FP8X4 = mybir.dt.float8_e4m3fn_x4
 MULT = mybir.AluOpType.mult
+COPY = mybir.ActivationFunctionType.Copy
 
 P = 128
 PACK = 4
 NB = N // P
-OC = C // 16
+CHUNKS = [128,128,128,128]
+FORMS = ["b","b","b","f"]
 
 
 def tile_routed_moe_kernel(tc, xT, w_words, w_scales, gate, offs, out):
@@ -29,18 +31,16 @@ def tile_routed_moe_kernel(tc, xT, w_words, w_scales, gate, offs, out):
         nc.sync.dma_start(offsets[:], offs)
 
         planes_dram = xT.rearrange("(p t) n -> p t n", t=PACK)
-        planes = []
+        raw = keep.tile([P, PACK, T], F32, name="raw")
         for t in range(PACK):
-            plane = keep.tile([P, T], F32, name="plane%d" % t)
-            nc.sync.dma_start(plane[:], planes_dram[:, t, :])
-            planes.append(plane)
+            nc.sync.dma_start(raw[:, t, :], planes_dram[:, t, :])
 
         w_plane = keep.tile([P, E, N], U8, name="w_plane", align_bytes=64)
         nc.vector.memset(w_plane[:].rearrange("p e n -> p (e n)").bitcast(I32), 0)
-        for q in range(4):
+        for q4 in range(4):
             nc.sync.dma_start(
-                w_plane[32 * q : 32 * q + 4, :, :].bitcast(I32),
-                w_scales[:, 0, 4 * q : 4 * q + 4, :].rearrange("e q n -> q e n").bitcast(I32),
+                w_plane[32 * q4 : 32 * q4 + 4, :, :].bitcast(I32),
+                w_scales[:, 0, 4 * q4 : 4 * q4 + 4, :].rearrange("e q n -> q e n").bitcast(I32),
             )
         w_codes = keep.tile([P, E, N], I32, name="w_codes", align_bytes=64)
         nc.sync.dma_start(w_codes[:], w_words.rearrange("e a p n r -> p (e a) (n r)").bitcast(I32))
@@ -54,74 +54,80 @@ def tile_routed_moe_kernel(tc, xT, w_words, w_scales, gate, offs, out):
         nc.scalar.copy(warm_out[:], warm_in[:])
 
         windows = [keep.tile([P, T], F32, name="window%d" % b) for b in range(NB)]
+        rounded = keep.tile([P, PACK, T], BF16, name="rounded")
 
-        gathered, grouped, codes, scales, sums, sums_sb = {}, {}, {}, {}, {}, {}
-        for e in range(E):
-            gathered[e] = keep.tile([P, PACK, C], F32, name="gathered%d" % e)
-            grouped[e] = keep.tile([P, C, PACK], BF16, name="grouped%d" % e, align_bytes=64)
-            codes[e] = keep.tile([P, C], I32, name="codes%d" % e, align_bytes=64)
-            scales[e] = keep.tile([P, C], U8, name="scales%d" % e, align_bytes=64)
-            sums[e] = psum.tile([P, NB, C], F32, name="sums%d" % e)
-            for b in range(NB):
-                sums_sb[e, b] = keep.tile([P, C], F32, name="sums_sb%d_%d" % (e, b))
+        starts = [sum(CHUNKS[:i]) for i in range(len(CHUNKS))]
+        grouped, sums_sb = {}, {}
 
-        def slots(e):
-            return offsets[:, e * OC : (e + 1) * OC]
+        def slots(i):
+            return offsets[:, starts[i] // 16 : (starts[i] + CHUNKS[i]) // 16]
 
-        def gather(e, t):
-            nc.vector.tensor_copy(gathered[e][:, t, :], planes[t][:].indirect(slots(e)))
+        def cast():
+            for t in range(PACK):
+                nc.scalar.copy(rounded[:, t, :], raw[:, t, :])
 
-        def interleave(e):
-            nc.scalar.copy(grouped[e][:], gathered[e][:].rearrange("p t c -> p c t"))
+        def g(i):
+            grouped[i] = keep.tile([P, CHUNKS[i], PACK], BF16, name="grouped%d" % i, align_bytes=64)
+            for t in range(PACK):
+                if FORMS[i] == "f":
+                    nc.scalar.activation(grouped[i][:, :, t], rounded[:, t, :].indirect(slots(i)), COPY)
+                else:
+                    nc.vector.tensor_copy(grouped[i][:, :, t], raw[:, t, :].indirect(slots(i)))
 
-        def quantise(e):
+        def q(i):
+            s0, n = starts[i], CHUNKS[i]
+            codes = keep.tile([P, n], I32, name="codes%d" % i, align_bytes=64)
+            scales = keep.tile([P, n], U8, name="scales%d" % i, align_bytes=64)
             nc.vector.quantize_mx(
-                out=codes[e][:].bitcast(FP8X4),
-                scales=scales[e][:],
-                in_=grouped[e][:].rearrange("p c t -> p (c t)"),
+                out=codes[:].bitcast(FP8X4),
+                scales=scales[:],
+                in_=grouped[i][:].rearrange("p c t -> p (c t)"),
             )
+            sums = psum.tile([P, NB, n], F32, name="sums%d" % i)
+            for e in range(E):
+                lo, hi = max(s0, e * C), min(s0 + n, (e + 1) * C)
+                if lo >= hi:
+                    continue
+                for b in range(NB):
+                    nc.tensor.matmul_mx(
+                        out=sums[:, b, lo - s0 : hi - s0],
+                        lhsT=w_codes[:, e, b * P : (b + 1) * P].bitcast(FP8X4),
+                        lhsT_scale=w_plane[:, e, b * P : (b + 1) * P],
+                        rhs=codes[:, lo - s0 : hi - s0].bitcast(FP8X4),
+                        rhs_scale=scales[:, lo - s0 : hi - s0],
+                        start=True,
+                        stop=True,
+                    )
+            sums_sb[i] = keep.tile([P, NB, n], F32, name="sums_sb%d" % i)
+            nc.scalar.copy(sums_sb[i][:], sums[:])
 
-        def multiply(e):
-            for b in range(NB):
-                nc.tensor.matmul_mx(
-                    out=sums[e][:, b, :],
-                    lhsT=w_codes[:, e, b * P : (b + 1) * P].bitcast(FP8X4),
-                    lhsT_scale=w_plane[:, e, b * P : (b + 1) * P],
-                    rhs=codes[e][:].bitcast(FP8X4),
-                    rhs_scale=scales[e][:],
-                    start=True,
-                    stop=True,
-                )
-
-        def empty(e):
-            for b in range(NB):
-                nc.scalar.copy(sums_sb[e, b][:], sums[e][:, b, :])
-
-        def scatter(e, b):
+        def s(i, b):
             nc.vector.tensor_tensor(
-                windows[b][:].indirect(slots(e)),
-                sums_sb[e, b][:],
-                gates[:, b, e * C : (e + 1) * C],
+                windows[b][:].indirect(slots(i)),
+                sums_sb[i][:, b, :],
+                gates[:, b, starts[i] : starts[i] + CHUNKS[i]],
                 MULT,
             )
 
-        for t in range(PACK):
-            gather(0, t)
-        interleave(0)
-        gather(1, 0)
-        gather(1, 1)
-        quantise(0)
-        multiply(0)
-        gather(1, 2)
-        gather(1, 3)
-        empty(0)
-        interleave(1)
-        scatter(0, 0)
-        quantise(1)
-        multiply(1)
-        empty(1)
-        scatter(0, 1)
-        scatter(1, 0)
-        nc.sync.dma_start(out[0:P, :], windows[0][:])
-        scatter(1, 1)
-        nc.sync.dma_start(out[P : 2 * P, :], windows[1][:])
+        def store(b):
+            nc.sync.dma_start(out[b * P : (b + 1) * P, :], windows[b][:])
+
+        g(0)
+        g(1)
+        q(0)
+        cast()
+        g(3)
+        g(2)
+        q(1)
+        q(2)
+        s(0, 0)
+        s(0, 1)
+        q(3)
+        s(1, 0)
+        s(1, 1)
+        s(2, 0)
+        s(2, 1)
+        s(3, 0)
+        store(0)
+        s(3, 1)
+        store(1)

@@ -26,6 +26,7 @@ def tile_routed_moe_kernel(tc, xT, w_words, w_scales, gate, offs, out):
     with ExitStack() as ctx:
         keep = ctx.enter_context(tc.tile_pool(name="keep", bufs=1))
         psum = ctx.enter_context(tc.psum_pool(name="psum", bufs=1))
+        gring = ctx.enter_context(tc.tile_pool(name="gring", bufs=2))
 
         offsets = keep.tile([P, E * C // 16], U16, name="offsets")
         nc.sync.dma_start(offsets[:], offs)
@@ -66,9 +67,13 @@ def tile_routed_moe_kernel(tc, xT, w_words, w_scales, gate, offs, out):
             for t in range(PACK):
                 nc.scalar.copy(rounded[:, t, :], raw[:, t, :])
 
-        def g(i):
-            grouped[i] = keep.tile([P, CHUNKS[i], PACK], BF16, name="grouped%d" % i, align_bytes=64)
-            for t in range(PACK):
+        def g(i, ts=(0, 1, 2, 3)):
+            if i not in grouped:
+                if FORMS[i] == "f":
+                    grouped[i] = keep.tile([P, CHUNKS[i], PACK], BF16, name="grouped_f%d" % i, align_bytes=64)
+                else:
+                    grouped[i] = gring.tile([P, CHUNKS[i], PACK], BF16, name="grouped", align_bytes=64)
+            for t in ts:
                 if FORMS[i] == "f":
                     nc.scalar.activation(grouped[i][:, :, t], rounded[:, t, :].indirect(slots(i)), COPY)
                 else:
@@ -120,9 +125,9 @@ def tile_routed_moe_kernel(tc, xT, w_words, w_scales, gate, offs, out):
         g(2)
         q(1)
         q(2)
+        q(3)
         s(0, 0)
         s(0, 1)
-        q(3)
         s(1, 0)
         s(1, 1)
         s(2, 0)

@@ -17,8 +17,9 @@ COPY = mybir.ActivationFunctionType.Copy
 P = 128
 PACK = 4
 NB = N // P
-CHUNKS = [128,128,128,128]
-FORMS = ["b","b","b","f"]
+CHUNKS = [128,128,64,64,128]
+FORMS = ["b","b","b","f","f"]
+GROUPS = [[0],[1],[2,3],[4]]
 
 
 def tile_routed_moe_kernel(tc, xT, w_words, w_scales, gate, offs, out):
@@ -58,7 +59,11 @@ def tile_routed_moe_kernel(tc, xT, w_words, w_scales, gate, offs, out):
         rounded = keep.tile([P, PACK, T], BF16, name="rounded")
 
         starts = [sum(CHUNKS[:i]) for i in range(len(CHUNKS))]
-        grouped, sums_sb = {}, {}
+        grouped, sums_sb, group_of = {}, {}, {}
+        for k in range(len(GROUPS)):
+            sums_sb[k] = keep.tile([P, NB, sum(CHUNKS[i] for i in GROUPS[k])], F32, name="sums_sb%d" % k)
+            for i in GROUPS[k]:
+                group_of[i] = k
 
         def slots(i):
             return offsets[:, starts[i] // 16 : (starts[i] + CHUNKS[i]) // 16]
@@ -103,14 +108,17 @@ def tile_routed_moe_kernel(tc, xT, w_words, w_scales, gate, offs, out):
                         start=True,
                         stop=True,
                     )
-            sums_sb[i] = keep.tile([P, NB, n], F32, name="sums_sb%d" % i)
-            nc.scalar.copy(sums_sb[i][:], sums[:])
+            k = group_of[i]
+            at = s0 - starts[GROUPS[k][0]]
+            nc.scalar.copy(sums_sb[k][:, :, at : at + n], sums[:])
 
-        def s(i, b):
+        def s(k, b):
+            lo = starts[GROUPS[k][0]]
+            hi = starts[GROUPS[k][-1]] + CHUNKS[GROUPS[k][-1]]
             nc.vector.tensor_tensor(
-                windows[b][:].indirect(slots(i)),
-                sums_sb[i][:, b, :],
-                gates[:, b, starts[i] : starts[i] + CHUNKS[i]],
+                windows[b][:].indirect(offsets[:, lo // 16 : hi // 16]),
+                sums_sb[k][:, b, :],
+                gates[:, b, lo:hi],
                 MULT,
             )
 
@@ -122,10 +130,12 @@ def tile_routed_moe_kernel(tc, xT, w_words, w_scales, gate, offs, out):
         q(0)
         cast()
         g(3)
+        g(4)
         g(2)
         q(1)
         q(2)
         q(3)
+        q(4)
         s(0, 0)
         s(0, 1)
         s(1, 0)

@@ -17,9 +17,8 @@ COPY = mybir.ActivationFunctionType.Copy
 P = 128
 PACK = 4
 NB = N // P
-CHUNKS = [128,128,64,64,128]
-FORMS = ["b","b","b","f","f"]
-GROUPS = [[0],[1],[2,3],[4]]
+CH = 128
+NCH = E * C // CH
 
 
 def tile_routed_moe_kernel(tc, xT, w_words, w_scales, gate, offs, out):
@@ -27,7 +26,6 @@ def tile_routed_moe_kernel(tc, xT, w_words, w_scales, gate, offs, out):
     with ExitStack() as ctx:
         keep = ctx.enter_context(tc.tile_pool(name="keep", bufs=1))
         psum = ctx.enter_context(tc.psum_pool(name="psum", bufs=1))
-        gring = ctx.enter_context(tc.tile_pool(name="gring", bufs=2))
 
         offsets = keep.tile([P, E * C // 16], U16, name="offsets")
         nc.sync.dma_start(offsets[:], offs)
@@ -47,8 +45,10 @@ def tile_routed_moe_kernel(tc, xT, w_words, w_scales, gate, offs, out):
         w_codes = keep.tile([P, E, N], I32, name="w_codes", align_bytes=64)
         nc.sync.dma_start(w_codes[:], w_words.rearrange("e a p n r -> p (e a) (n r)").bitcast(I32))
 
-        gates = keep.tile([P, NB, E * C], F32, name="gates")
-        nc.sync.dma_start(gates[:], gate.rearrange("(b p) j -> p b j", p=P))
+        gate_dram = gate.rearrange("(b p) j -> p b j", p=P)
+        gates = [keep.tile([P, NB, C], F32, name="gates%d" % e) for e in range(E)]
+        for e in range(E):
+            nc.sync.dma_start(gates[e][:], gate_dram[:, :, e * C : (e + 1) * C])
 
         warm_in = keep.tile([P, 1], F32, name="warm_in")
         warm_out = keep.tile([P, 1], F32, name="warm_out")
@@ -56,88 +56,90 @@ def tile_routed_moe_kernel(tc, xT, w_words, w_scales, gate, offs, out):
         nc.scalar.copy(warm_out[:], warm_in[:])
 
         windows = [keep.tile([P, T], F32, name="window%d" % b) for b in range(NB)]
-        rounded = keep.tile([P, PACK, T], BF16, name="rounded")
+        rounded_g = keep.tile([P, 2, T], BF16, name="rounded_g")
+        rounded_s = keep.tile([P, 2, T], BF16, name="rounded_s")
 
-        starts = [sum(CHUNKS[:i]) for i in range(len(CHUNKS))]
-        grouped, sums_sb, group_of = {}, {}, {}
-        for k in range(len(GROUPS)):
-            sums_sb[k] = keep.tile([P, NB, sum(CHUNKS[i] for i in GROUPS[k])], F32, name="sums_sb%d" % k)
-            for i in GROUPS[k]:
-                group_of[i] = k
+        def plane(t):
+            return rounded_g[:, t - 1, :] if t in (1, 2) else rounded_s[:, t // 3, :]
+
+        grouped, sums, sums_sb = {}, {}, {}
 
         def slots(i):
-            return offsets[:, starts[i] // 16 : (starts[i] + CHUNKS[i]) // 16]
+            return offsets[:, i * CH // 16 : (i + 1) * CH // 16]
 
-        def cast():
-            for t in range(PACK):
-                nc.scalar.copy(rounded[:, t, :], raw[:, t, :])
+        def cast(t):
+            if t in (1, 2):
+                nc.gpsimd.tensor_copy(plane(t), raw[:, t, :])
+            else:
+                nc.scalar.copy(plane(t), raw[:, t, :])
 
-        def g(i, ts=(0, 1, 2, 3)):
-            if i not in grouped:
-                if FORMS[i] == "f":
-                    grouped[i] = keep.tile([P, CHUNKS[i], PACK], BF16, name="grouped_f%d" % i, align_bytes=64)
-                else:
-                    grouped[i] = gring.tile([P, CHUNKS[i], PACK], BF16, name="grouped", align_bytes=64)
-            for t in ts:
-                if FORMS[i] == "f":
-                    nc.scalar.activation(grouped[i][:, :, t], rounded[:, t, :].indirect(slots(i)), COPY)
-                else:
-                    nc.vector.tensor_copy(grouped[i][:, :, t], raw[:, t, :].indirect(slots(i)))
+        def alloc(i, tag):
+            grouped[i] = keep.tile([P, CH, PACK], BF16, name="grouped%d" % i, tag=tag, align_bytes=64)
 
-        def q(i):
-            s0, n = starts[i], CHUNKS[i]
-            codes = keep.tile([P, n], I32, name="codes%d" % i, align_bytes=64)
-            scales = keep.tile([P, n], U8, name="scales%d" % i, align_bytes=64)
+        def gv(i, t):
+            nc.vector.tensor_copy(grouped[i][:, :, t], raw[:, t, :].indirect(slots(i)))
+
+        def gs(i, t):
+            nc.scalar.activation(grouped[i][:, :, t], plane(t).indirect(slots(i)), COPY)
+
+        def q(i, tag):
+            codes = keep.tile([P, CH], I32, name="codes%d" % i, tag=tag, align_bytes=64)
+            scales = keep.tile([P, CH], U8, name="scales%d" % i, align_bytes=64)
             nc.vector.quantize_mx(
                 out=codes[:].bitcast(FP8X4),
                 scales=scales[:],
                 in_=grouped[i][:].rearrange("p c t -> p (c t)"),
             )
-            sums = psum.tile([P, NB, n], F32, name="sums%d" % i)
-            for e in range(E):
-                lo, hi = max(s0, e * C), min(s0 + n, (e + 1) * C)
-                if lo >= hi:
-                    continue
-                for b in range(NB):
-                    nc.tensor.matmul_mx(
-                        out=sums[:, b, lo - s0 : hi - s0],
-                        lhsT=w_codes[:, e, b * P : (b + 1) * P].bitcast(FP8X4),
-                        lhsT_scale=w_plane[:, e, b * P : (b + 1) * P],
-                        rhs=codes[:, lo - s0 : hi - s0].bitcast(FP8X4),
-                        rhs_scale=scales[:, lo - s0 : hi - s0],
-                        start=True,
-                        stop=True,
-                    )
-            k = group_of[i]
-            at = s0 - starts[GROUPS[k][0]]
-            nc.scalar.copy(sums_sb[k][:, :, at : at + n], sums[:])
+            sums[i] = psum.tile([P, NB, CH], F32, name="sums%d" % i)
+            e = i * CH // C
+            for b in range(NB):
+                nc.tensor.matmul_mx(
+                    out=sums[i][:, b, :],
+                    lhsT=w_codes[:, e, b * P : (b + 1) * P].bitcast(FP8X4),
+                    lhsT_scale=w_plane[:, e, b * P : (b + 1) * P],
+                    rhs=codes[:].bitcast(FP8X4),
+                    rhs_scale=scales[:],
+                    start=True,
+                    stop=True,
+                )
 
-        def s(k, b):
-            lo = starts[GROUPS[k][0]]
-            hi = starts[GROUPS[k][-1]] + CHUNKS[GROUPS[k][-1]]
+        def c(i, tag):
+            sums_sb[i] = keep.tile([P, NB, CH], F32, name="sums_sb%d" % i, tag=tag, align_bytes=64)
+            nc.scalar.copy(sums_sb[i][:], sums[i][:])
+
+        def s(i, b):
             nc.vector.tensor_tensor(
-                windows[b][:].indirect(offsets[:, lo // 16 : hi // 16]),
-                sums_sb[k][:, b, :],
-                gates[:, b, lo:hi],
+                windows[b][:].indirect(slots(i)),
+                sums_sb[i][:, b, :],
+                gates[i * CH // C][:, b, i * CH % C : i * CH % C + CH],
                 MULT,
             )
 
         def store(b):
             nc.sync.dma_start(out[b * P : (b + 1) * P, :], windows[b][:])
 
-        g(0)
-        g(1)
-        q(0)
-        cast()
-        g(3)
-        g(4)
-        g(2)
-        q(1)
-        q(2)
-        q(3)
-        q(4)
+        alloc(0, "g0")
+        alloc(1, "g1")
+        for t in range(PACK):
+            gv(0, t)
+            gv(1, t)
+            cast(t)
+        q(0, "c0")
+        q(1, "c1")
+        alloc(2, "g2")
+        for t in range(PACK):
+            gs(2, t)
+        c(0, "b0")
+        c(1, "b1")
+        alloc(3, "c0")
+        for t in range(PACK):
+            gs(3, t)
+        q(2, "c2")
+        c(2, "b2")
         s(0, 0)
         s(0, 1)
+        q(3, "b0")
+        c(3, "b3")
         s(1, 0)
         s(1, 1)
         s(2, 0)

@@ -131,7 +131,7 @@ def tile_routed_moe_kernel(tc, xT, w_words, w_scales, gate, offs, out):
             gs(2, t)
         c(0, "b0")
         c(1, "b1")
-        alloc(3, "c0")
+        alloc(3, "c1")
         for t in range(PACK):
             gs(3, t)
         q(2, "c2")

@@ -131,10 +131,10 @@ def tile_routed_moe_kernel(tc, xT, w_words, w_scales, gate, offs, out):
             gs(2, t)
         c(0, "b0")
         c(1, "b1")
-        alloc(3, "c1")
+        q(2, "c2")
+        alloc(3, "c2")
         for t in range(PACK):
             gs(3, t)
-        q(2, "c2")
         c(2, "b2")
         s(0, 0)
         s(0, 1)

@@ -17,8 +17,9 @@ COPY = mybir.ActivationFunctionType.Copy
 P = 128
 PACK = 4
 NB = N // P
-CH = 128
-NCH = E * C // CH
+SIZES = [128, 64, 64, 128, 128]
+STARTS = [0, 128, 192, 256, 384]
+PIECE = [0, 1, 1, 2, 3]
 
 
 def tile_routed_moe_kernel(tc, xT, w_words, w_scales, gate, offs, out):
@@ -64,8 +65,8 @@ def tile_routed_moe_kernel(tc, xT, w_words, w_scales, gate, offs, out):
 
         grouped, sums, sums_sb = {}, {}, {}
 
-        def slots(i):
-            return offsets[:, i * CH // 16 : (i + 1) * CH // 16]
+        def slots(lo, n):
+            return offsets[:, lo // 16 : (lo + n) // 16]
 
         def cast(t):
             if t in (1, 2):
@@ -74,24 +75,25 @@ def tile_routed_moe_kernel(tc, xT, w_words, w_scales, gate, offs, out):
                 nc.scalar.copy(plane(t), raw[:, t, :])
 
         def alloc(i, tag):
-            grouped[i] = keep.tile([P, CH, PACK], BF16, name="grouped%d" % i, tag=tag, align_bytes=64)
+            grouped[i] = keep.tile([P, SIZES[i], PACK], BF16, name="grouped%d" % i, tag=tag, align_bytes=64)
 
         def gv(i, t):
-            nc.vector.tensor_copy(grouped[i][:, :, t], raw[:, t, :].indirect(slots(i)))
+            nc.vector.tensor_copy(grouped[i][:, :, t], raw[:, t, :].indirect(slots(STARTS[i], SIZES[i])))
 
         def gs(i, t):
-            nc.scalar.activation(grouped[i][:, :, t], plane(t).indirect(slots(i)), COPY)
+            nc.scalar.activation(grouped[i][:, :, t], plane(t).indirect(slots(STARTS[i], SIZES[i])), COPY)
 
         def q(i, tag):
-            codes = keep.tile([P, CH], I32, name="codes%d" % i, tag=tag, align_bytes=64)
-            scales = keep.tile([P, CH], U8, name="scales%d" % i, align_bytes=64)
+            n = SIZES[i]
+            codes = keep.tile([P, n], I32, name="codes%d" % i, tag=tag, align_bytes=64)
+            scales = keep.tile([P, n], U8, name="scales%d" % i, align_bytes=64)
             nc.vector.quantize_mx(
                 out=codes[:].bitcast(FP8X4),
                 scales=scales[:],
                 in_=grouped[i][:].rearrange("p c t -> p (c t)"),
             )
-            sums[i] = psum.tile([P, NB, CH], F32, name="sums%d" % i)
-            e = i * CH // C
+            sums[i] = psum.tile([P, NB, n], F32, name="sums%d" % i)
+            e = STARTS[i] // C
             for b in range(NB):
                 nc.tensor.matmul_mx(
                     out=sums[i][:, b, :],
@@ -103,15 +105,19 @@ def tile_routed_moe_kernel(tc, xT, w_words, w_scales, gate, offs, out):
                     stop=True,
                 )
 
-        def c(i, tag):
-            sums_sb[i] = keep.tile([P, NB, CH], F32, name="sums_sb%d" % i, tag=tag, align_bytes=64)
-            nc.scalar.copy(sums_sb[i][:], sums[i][:])
+        def c(i):
+            k = PIECE[i]
+            if k not in sums_sb:
+                sums_sb[k] = keep.tile([P, NB, 128], F32, name="sums_sb%d" % k, tag="b%d" % k, align_bytes=64)
+            at = STARTS[i] - 128 * k
+            nc.scalar.copy(sums_sb[k][:, :, at : at + SIZES[i]], sums[i][:])
 
-        def s(i, b):
+        def s(k, b):
+            lo = 128 * k
             nc.vector.tensor_tensor(
-                windows[b][:].indirect(slots(i)),
-                sums_sb[i][:, b, :],
-                gates[i * CH // C][:, b, i * CH % C : i * CH % C + CH],
+                windows[b][:].indirect(slots(lo, 128)),
+                sums_sb[k][:, b, :],
+                gates[lo // C][:, b, lo % C : lo % C + 128],
                 MULT,
             )
 
@@ -129,17 +135,22 @@ def tile_routed_moe_kernel(tc, xT, w_words, w_scales, gate, offs, out):
         alloc(2, "g2")
         for t in range(PACK):
             gs(2, t)
-        c(0, "b0")
-        c(1, "b1")
-        q(2, "c2")
-        alloc(3, "c2")
+        alloc(3, "g3")
         for t in range(PACK):
             gs(3, t)
-        c(2, "b2")
+        c(0)
+        c(1)
+        q(2, "c2")
+        c(2)
+        q(3, "c3")
+        alloc(4, "c2")
+        for t in range(PACK):
+            gs(4, t)
+        c(3)
         s(0, 0)
         s(0, 1)
-        q(3, "b0")
-        c(3, "b3")
+        q(4, "b0")
+        c(4)
         s(1, 0)
         s(1, 1)
         s(2, 0)

@@ -17,9 +17,6 @@ COPY = mybir.ActivationFunctionType.Copy
 P = 128
 PACK = 4
 NB = N // P
-SIZES = [128, 64, 64, 128, 128]
-STARTS = [0, 128, 192, 256, 384]
-PIECE = [0, 1, 1, 2, 3]
 
 
 def tile_routed_moe_kernel(tc, xT, w_words, w_scales, gate, offs, out):
@@ -74,29 +71,31 @@ def tile_routed_moe_kernel(tc, xT, w_words, w_scales, gate, offs, out):
             else:
                 nc.scalar.copy(plane(t), raw[:, t, :])
 
-        def alloc(i, tag):
-            grouped[i] = keep.tile([P, SIZES[i], PACK], BF16, name="grouped%d" % i, tag=tag, align_bytes=64)
+        def alloc(lo, n, tag):
+            grouped[lo] = (keep.tile([P, n, PACK], BF16, name="grouped%d" % lo, tag=tag, align_bytes=64), n)
 
-        def gv(i, t):
-            nc.vector.tensor_copy(grouped[i][:, :, t], raw[:, t, :].indirect(slots(STARTS[i], SIZES[i])))
+        def gv(lo, t):
+            tile, n = grouped[lo]
+            nc.vector.tensor_copy(tile[:, :, t], raw[:, t, :].indirect(slots(lo, n)))
 
-        def gs(i, t):
-            nc.scalar.activation(grouped[i][:, :, t], plane(t).indirect(slots(STARTS[i], SIZES[i])), COPY)
+        def gs(lo, t):
+            tile, n = grouped[lo]
+            nc.scalar.activation(tile[:, :, t], plane(t).indirect(slots(lo, n)), COPY)
 
-        def q(i, tag):
-            n = SIZES[i]
-            codes = keep.tile([P, n], I32, name="codes%d" % i, tag=tag, align_bytes=64)
-            scales = keep.tile([P, n], U8, name="scales%d" % i, align_bytes=64)
+        def q(glo, lo, n, tag):
+            tile = grouped[glo][0]
+            codes = keep.tile([P, n], I32, name="codes%d" % lo, tag=tag, align_bytes=64)
+            scales = keep.tile([P, n], U8, name="scales%d" % lo, align_bytes=64)
             nc.vector.quantize_mx(
                 out=codes[:].bitcast(FP8X4),
                 scales=scales[:],
-                in_=grouped[i][:].rearrange("p c t -> p (c t)"),
+                in_=tile[:, lo - glo : lo - glo + n, :].rearrange("p c t -> p (c t)"),
             )
-            sums[i] = psum.tile([P, NB, n], F32, name="sums%d" % i)
-            e = STARTS[i] // C
+            sums[lo] = (psum.tile([P, NB, n], F32, name="sums%d" % lo), n)
+            e = lo // C
             for b in range(NB):
                 nc.tensor.matmul_mx(
-                    out=sums[i][:, b, :],
+                    out=sums[lo][0][:, b, :],
                     lhsT=w_codes[:, e, b * P : (b + 1) * P].bitcast(FP8X4),
                     lhsT_scale=w_plane[:, e, b * P : (b + 1) * P],
                     rhs=codes[:].bitcast(FP8X4),
@@ -105,12 +104,16 @@ def tile_routed_moe_kernel(tc, xT, w_words, w_scales, gate, offs, out):
                     stop=True,
                 )
 
-        def c(i):
-            k = PIECE[i]
+        def c(lo, eng="s"):
+            k = lo // 128
             if k not in sums_sb:
                 sums_sb[k] = keep.tile([P, NB, 128], F32, name="sums_sb%d" % k, tag="b%d" % k, align_bytes=64)
-            at = STARTS[i] - 128 * k
-            nc.scalar.copy(sums_sb[k][:, :, at : at + SIZES[i]], sums[i][:])
+            at = lo - 128 * k
+            src, n = sums[lo]
+            if eng == "v":
+                nc.vector.tensor_copy(sums_sb[k][:, :, at : at + n], src[:])
+            else:
+                nc.scalar.copy(sums_sb[k][:, :, at : at + n], src[:])
 
         def s(k, b):
             lo = 128 * k
@@ -124,33 +127,28 @@ def tile_routed_moe_kernel(tc, xT, w_words, w_scales, gate, offs, out):
         def store(b):
             nc.sync.dma_start(out[b * P : (b + 1) * P, :], windows[b][:])
 
-        alloc(0, "g0")
-        alloc(1, "g1")
+        alloc(0, 192, "g0")
         for t in range(PACK):
             gv(0, t)
-            gv(1, t)
             cast(t)
-        q(0, "c0")
-        q(1, "c1")
-        alloc(2, "g2")
+        q(0, 0, 128, "c0")
+        q(0, 128, 64, "c1")
+        alloc(192, 192, "g2")
         for t in range(PACK):
-            gs(2, t)
-        alloc(3, "g3")
-        for t in range(PACK):
-            gs(3, t)
+            gs(192, t)
         c(0)
-        c(1)
-        q(2, "c2")
-        c(2)
-        q(3, "c3")
-        alloc(4, "c2")
+        c(128)
+        q(192, 192, 64, "c2")
+        c(192)
+        q(192, 256, 128, "c3")
+        alloc(384, 128, "c2")
         for t in range(PACK):
-            gs(4, t)
-        c(3)
+            gs(384, t)
+        c(256)
         s(0, 0)
         s(0, 1)
-        q(4, "b0")
-        c(4)
+        q(384, 384, 128, "b0")
+        c(384)
         s(1, 0)
         s(1, 1)
         s(2, 0)

@@ -54,11 +54,11 @@ def tile_routed_moe_kernel(tc, xT, w_words, w_scales, gate, offs, out):
         nc.scalar.copy(warm_out[:], warm_in[:])
 
         windows = [keep.tile([P, T], F32, name="window%d" % b) for b in range(NB)]
-        rounded_g = keep.tile([P, 2, T], BF16, name="rounded_g")
-        rounded_s = keep.tile([P, 2, T], BF16, name="rounded_s")
+        rounded_g = keep.tile([P, 3, T], BF16, name="rounded_g")
+        rounded_s = keep.tile([P, 1, T], BF16, name="rounded_s")
 
         def plane(t):
-            return rounded_g[:, t - 1, :] if t in (1, 2) else rounded_s[:, t // 3, :]
+            return rounded_g[:, t - 1, :] if t > 0 else rounded_s[:, 0, :]
 
         grouped, sums, sums_sb = {}, {}, {}
 
@@ -66,7 +66,7 @@ def tile_routed_moe_kernel(tc, xT, w_words, w_scales, gate, offs, out):
             return offsets[:, lo // 16 : (lo + n) // 16]
 
         def cast(t):
-            if t in (1, 2):
+            if t in (1, 2, 3):
                 nc.gpsimd.tensor_copy(plane(t), raw[:, t, :])
             else:
                 nc.scalar.copy(plane(t), raw[:, t, :])

@@ -26,11 +26,12 @@ def tile_routed_moe_kernel(tc, xT, w_words, w_scales, gate, offs, out):
         psum = ctx.enter_context(tc.psum_pool(name="psum", bufs=1))
 
         offsets = keep.tile([P, E * C // 16], U16, name="offsets")
-        nc.sync.dma_start(offsets[:], offs)
 
         planes_dram = xT.rearrange("(p t) n -> p t n", t=PACK)
         raw = keep.tile([P, PACK, T], F32, name="raw")
-        for t in range(PACK):
+        nc.sync.dma_start(raw[:, 0, :], planes_dram[:, 0, :])
+        nc.sync.dma_start(offsets[:], offs)
+        for t in range(1, PACK):
             nc.sync.dma_start(raw[:, t, :], planes_dram[:, t, :])
 
         w_plane = keep.tile([P, E, N], U8, name="w_plane", align_bytes=64)

@@ -79,6 +79,10 @@ def tile_routed_moe_kernel(tc, xT, w_words, w_scales, gate, offs, out):
             tile, n = grouped[lo]
             nc.vector.tensor_copy(tile[:, :, t], raw[:, t, :].indirect(slots(lo, n)))
 
+        def gv_part(glo, lo, n, t):
+            tile = grouped[glo][0]
+            nc.vector.tensor_copy(tile[:, lo - glo : lo - glo + n, t], raw[:, t, :].indirect(slots(lo, n)))
+
         def gs(lo, t):
             tile, n = grouped[lo]
             nc.scalar.activation(tile[:, :, t], plane(t).indirect(slots(lo, n)), COPY)
@@ -129,9 +133,12 @@ def tile_routed_moe_kernel(tc, xT, w_words, w_scales, gate, offs, out):
             nc.sync.dma_start(out[b * P : (b + 1) * P, :], windows[b][:])
 
         alloc(0, 192, "g0")
-        for t in range(PACK):
+        for t in range(PACK - 1):
             gv(0, t)
             cast(t)
+        gv_part(0, 0, 128, PACK - 1)
+        gv_part(0, 128, 64, PACK - 1)
+        cast(PACK - 1)
         q(0, 0, 128, "c0")
         q(0, 128, 64, "c1")
         alloc(192, 192, "g2")

@@ -34,6 +34,9 @@ def tile_routed_moe_kernel(tc, xT, w_words, w_scales, gate, offs, out):
         for t in range(1, PACK):
             nc.sync.dma_start(raw[:, t, :], planes_dram[:, t, :])
 
+        w_codes = keep.tile([P, E, N], I32, name="w_codes", align_bytes=64)
+        nc.sync.dma_start(w_codes[:], w_words.rearrange("e a p n r -> p (e a) (n r)").bitcast(I32))
+
         w_plane = keep.tile([P, E, N], U8, name="w_plane", align_bytes=64)
         nc.vector.memset(w_plane[:].rearrange("p e n -> p (e n)").bitcast(I32), 0)
         for q4 in range(4):
@@ -41,8 +44,6 @@ def tile_routed_moe_kernel(tc, xT, w_words, w_scales, gate, offs, out):
                 w_plane[32 * q4 : 32 * q4 + 4, :, :].bitcast(I32),
                 w_scales[:, 0, 4 * q4 : 4 * q4 + 4, :].rearrange("e q n -> q e n").bitcast(I32),
             )
-        w_codes = keep.tile([P, E, N], I32, name="w_codes", align_bytes=64)
-        nc.sync.dma_start(w_codes[:], w_words.rearrange("e a p n r -> p (e a) (n r)").bitcast(I32))
 
         gate_dram = gate.rearrange("(b p) j -> p b j", p=P)
         gates = [keep.tile([P, NB, C], F32, name="gates%d" % e) for e in range(E)]

@@ -88,6 +88,10 @@ def tile_routed_moe_kernel(tc, xT, w_words, w_scales, gate, offs, out):
             tile, n = grouped[lo]
             nc.scalar.activation(tile[:, :, t], plane(t).indirect(slots(lo, n)), COPY)
 
+        def gs_part(glo, lo, n, t):
+            tile = grouped[glo][0]
+            nc.scalar.activation(tile[:, lo - glo : lo - glo + n, t], plane(t).indirect(slots(lo, n)), COPY)
+
         def q(glo, lo, n, tag):
             tile = grouped[glo][0]
             codes = keep.tile([P, n], I32, name="codes%d" % lo, tag=tag, align_bytes=64)
@@ -134,17 +138,21 @@ def tile_routed_moe_kernel(tc, xT, w_words, w_scales, gate, offs, out):
             nc.sync.dma_start(out[b * P : (b + 1) * P, :], windows[b][:])
 
         alloc(0, 192, "g0")
-        for t in range(PACK - 1):
-            gv(0, t)
+        for t in range(2):
+            gv_part(0, 0, 128, t)
             cast(t)
+            gs_part(0, 128, 64, t)
+        gv(0, 2)
+        cast(2)
         gv_part(0, 0, 128, PACK - 1)
         gv_part(0, 128, 64, PACK - 1)
         cast(PACK - 1)
         q(0, 0, 128, "c0")
         q(0, 128, 64, "c1")
         alloc(192, 192, "g2")
-        for t in range(PACK):
+        for t in range(PACK - 1):
             gs(192, t)
+        gs(192, PACK - 1)
         c(0)
         c(128)
         q(192, 192, 64, "c2")

@@ -125,6 +125,12 @@ def tile_routed_moe_kernel(tc, xT, w_words, w_scales, gate, offs, out):
             else:
                 nc.scalar.copy(sums_sb[k][:, :, at : at + n], src[:])
 
+        def c_block(lo, b):
+            k = lo // 128
+            if k not in sums_sb:
+                sums_sb[k] = keep.tile([P, NB, 128], F32, name="sums_sb%d" % k, tag="b%d" % k, align_bytes=64)
+            nc.scalar.copy(sums_sb[k][:, b, :], sums[lo][0][:, b, :])
+
         def s(k, b):
             lo = 128 * k
             nc.vector.tensor_tensor(
@@ -152,8 +158,10 @@ def tile_routed_moe_kernel(tc, xT, w_words, w_scales, gate, offs, out):
         alloc(192, 192, "g2")
         for t in range(PACK - 1):
             gs(192, t)
-        gs(192, PACK - 1)
-        c(0)
+        gs_part(192, 192, 64, PACK - 1)
+        gs_part(192, 256, 128, PACK - 1)
+        c_block(0, 0)
+        c_block(0, 1)
         c(128)
         q(192, 192, 64, "c2")
         c(192)

from contextlib import ExitStack

import concourse.mybir as mybir

K, T, E, C, N = 512, 512, 2, 256, 256
FLOPS = 2 * K * N * E * C

F32 = mybir.dt.float32
BF16 = mybir.dt.bfloat16
I32 = mybir.dt.int32
U16 = mybir.dt.uint16
U8 = mybir.dt.uint8
FP8X4 = mybir.dt.float8_e4m3fn_x4
MULT = mybir.AluOpType.mult
COPY = mybir.ActivationFunctionType.Copy

P = 128
PACK = 4
NB = N // P


def tile_routed_moe_kernel(tc, xT, w_words, w_scales, gate, offs, out):
    nc = tc.nc
    with ExitStack() as ctx:
        keep = ctx.enter_context(tc.tile_pool(name="keep", bufs=1))
        psum = ctx.enter_context(tc.psum_pool(name="psum", bufs=1))

        offsets = keep.tile([P, E * C // 16], U16, name="offsets")

        planes_dram = xT.rearrange("(p t) n -> p t n", t=PACK)
        raw = keep.tile([P, PACK, T], F32, name="raw")
        nc.sync.dma_start(raw[:, 0, :], planes_dram[:, 0, :])
        nc.sync.dma_start(offsets[:], offs)
        for t in range(1, PACK):
            nc.sync.dma_start(raw[:, t, :], planes_dram[:, t, :])

        w_codes = keep.tile([P, E, N], I32, name="w_codes", align_bytes=64)
        nc.sync.dma_start(w_codes[:], w_words.rearrange("e a p n r -> p (e a) (n r)").bitcast(I32))

        w_plane = keep.tile([P, E, N], U8, name="w_plane", align_bytes=64)
        nc.vector.memset(w_plane[:].rearrange("p e n -> p (e n)").bitcast(I32), 0)
        for q4 in range(4):
            nc.sync.dma_start(
                w_plane[32 * q4 : 32 * q4 + 4, :, :].bitcast(I32),
                w_scales[:, 0, 4 * q4 : 4 * q4 + 4, :].rearrange("e q n -> q e n").bitcast(I32),
            )

        gate_dram = gate.rearrange("(b p) j -> p b j", p=P)
        gates = [keep.tile([P, NB, C], F32, name="gates%d" % e) for e in range(E)]
        for e in range(E):
            nc.sync.dma_start(gates[e][:], gate_dram[:, :, e * C : (e + 1) * C])

        warm_in = keep.tile([P, 1], F32, name="warm_in")
        warm_out = keep.tile([P, 1], F32, name="warm_out")
        nc.vector.memset(warm_in[:], 0.0)
        nc.scalar.copy(warm_out[:], warm_in[:])

        windows = [keep.tile([P, T], F32, name="window%d" % b) for b in range(NB)]
        rounded_g = keep.tile([P, 3, T], BF16, name="rounded_g")
        rounded_s = keep.tile([P, 1, T], BF16, name="rounded_s")

        def plane(t):
            return rounded_g[:, t - 1, :] if t > 0 else rounded_s[:, 0, :]

        grouped, sums, sums_sb = {}, {}, {}

        def slots(lo, n):
            return offsets[:, lo // 16 : (lo + n) // 16]

        def cast(t):
            if t in (1, 2, 3):
                nc.gpsimd.tensor_copy(plane(t), raw[:, t, :])
            else:
                nc.scalar.copy(plane(t), raw[:, t, :])

        def alloc(lo, n, tag):
            grouped[lo] = (keep.tile([P, n, PACK], BF16, name="grouped%d" % lo, tag=tag, align_bytes=64), n)

        def gv(lo, t):
            tile, n = grouped[lo]
            nc.vector.tensor_copy(tile[:, :, t], raw[:, t, :].indirect(slots(lo, n)))

        def gv_part(glo, lo, n, t):
            tile = grouped[glo][0]
            nc.vector.tensor_copy(tile[:, lo - glo : lo - glo + n, t], raw[:, t, :].indirect(slots(lo, n)))

        def gs(lo, t):
            tile, n = grouped[lo]
            nc.scalar.activation(tile[:, :, t], plane(t).indirect(slots(lo, n)), COPY)

        def gs_part(glo, lo, n, t):
            tile = grouped[glo][0]
            nc.scalar.activation(tile[:, lo - glo : lo - glo + n, t], plane(t).indirect(slots(lo, n)), COPY)

        def q(glo, lo, n, tag):
            tile = grouped[glo][0]
            codes = keep.tile([P, n], I32, name="codes%d" % lo, tag=tag, align_bytes=64)
            scales = keep.tile([P, n], U8, name="scales%d" % lo, align_bytes=64)
            nc.vector.quantize_mx(
                out=codes[:].bitcast(FP8X4),
                scales=scales[:],
                in_=tile[:, lo - glo : lo - glo + n, :].rearrange("p c t -> p (c t)"),
            )
            sums[lo] = (psum.tile([P, NB, n], F32, name="sums%d" % lo), n)
            e = lo // C
            for b in range(NB):
                nc.tensor.matmul_mx(
                    out=sums[lo][0][:, b, :],
                    lhsT=w_codes[:, e, b * P : (b + 1) * P].bitcast(FP8X4),
                    lhsT_scale=w_plane[:, e, b * P : (b + 1) * P],
                    rhs=codes[:].bitcast(FP8X4),
                    rhs_scale=scales[:],
                    start=True,
                    stop=True,
                )

        def c(lo, eng="s"):
            k = lo // 128
            if k not in sums_sb:
                sums_sb[k] = keep.tile([P, NB, 128], F32, name="sums_sb%d" % k, tag="b%d" % k, align_bytes=64)
            at = lo - 128 * k
            src, n = sums[lo]
            if eng == "v":
                nc.vector.tensor_copy(sums_sb[k][:, :, at : at + n], src[:])
            else:
                nc.scalar.copy(sums_sb[k][:, :, at : at + n], src[:])

        def c_block(lo, b):
            k = lo // 128
            if k not in sums_sb:
                sums_sb[k] = keep.tile([P, NB, 128], F32, name="sums_sb%d" % k, tag="b%d" % k, align_bytes=64)
            nc.scalar.copy(sums_sb[k][:, b, :], sums[lo][0][:, b, :])

        def s(k, b):
            lo = 128 * k
            nc.vector.tensor_tensor(
                windows[b][:].indirect(slots(lo, 128)),
                sums_sb[k][:, b, :],
                gates[lo // C][:, b, lo % C : lo % C + 128],
                MULT,
            )

        def store(b):
            nc.sync.dma_start(out[b * P : (b + 1) * P, :], windows[b][:])

        alloc(0, 192, "g0")
        for t in range(2):
            gv_part(0, 0, 128, t)
            cast(t)
            gs_part(0, 128, 64, t)
        gv(0, 2)
        cast(2)
        gv_part(0, 0, 128, PACK - 1)
        gv_part(0, 128, 64, PACK - 1)
        cast(PACK - 1)
        q(0, 0, 128, "c0")
        q(0, 128, 64, "c1")
        alloc(192, 192, "g2")
        for t in range(PACK - 1):
            gs(192, t)
        gs_part(192, 192, 64, PACK - 1)
        gs_part(192, 256, 128, PACK - 1)
        c_block(0, 0)
        c_block(0, 1)
        c(128)
        q(192, 192, 64, "c2")
        c(192)
        q(192, 256, 128, "c3")
        alloc(384, 128, "c2")
        for t in range(PACK):
            gs(384, t)
        c(256)
        s(0, 0)
        s(0, 1)
        q(384, 384, 128, "b0")
        c(384)
        s(1, 0)
        s(1, 1)
        s(2, 0)
        s(2, 1)
        s(3, 0)
        store(0)
        s(3, 1)
        store(1)
